import numpy as np
import ml_dtypes


def mxq(x, axis, fmt="e4m3"):
    dtype, down = {"e4m3": (ml_dtypes.float8_e4m3fn, 7), "e5m2": (ml_dtypes.float8_e5m2, 14)}[fmt]
    v = np.moveaxis(np.asarray(x, np.float32).astype(ml_dtypes.bfloat16).astype(np.float64), axis, -1)
    blocks = v.reshape(v.shape[:-1] + (-1, 32))
    amax = np.abs(blocks).max(-1, keepdims=True)
    byte = np.maximum(np.where(amax > 0, np.frexp(amax)[1] - 1 + 127, 0) - down, 1)
    scale = np.exp2(byte - 127.0)
    codes = (blocks / scale).astype(np.float32).astype(dtype).astype(np.float64)
    return np.moveaxis((codes * scale).reshape(v.shape), -1, axis)


WIDE = False


def mx_kscale(k):
    if not WIDE:
        return np.ones(k)
    levels = np.array([30, -30])
    if k % 512:
        return np.exp2(np.random.permutation(np.resize(levels, k // 32))).repeat(32)
    a = np.empty((k // 512, 16))
    for p in range(k // 512):
        a[p, :8] = np.random.permutation(np.resize(levels, 8))
        for g in range(8):
            far = levels[np.abs(levels - a[p, g]) >= 10]
            a[p, g + 8] = far[np.random.randint(len(far))]
    return np.exp2(a.ravel()).repeat(32)


def f64(x):
    return np.asarray(x).astype(np.float64)


def striped(idx):
    return np.tile(np.asarray(idx).reshape(-1, 16).T, (8, 1)).astype(np.uint16)


def unstriped(offs):
    return offs[:16].T.reshape(-1).astype(np.int64)


E2M1 = np.array([0.0, 0.5, 1.0, 1.5, 2.0, 3.0, 4.0, 6.0, -0.0, -0.5, -1.0, -1.5, -2.0, -3.0, -4.0, -6.0])


def pack_weight(w, fmt):
    k, n = w.shape
    w = f64(np.asarray(w, np.float32).astype(ml_dtypes.bfloat16)).reshape(k // 32, 32, n)
    amax = np.abs(w).max(1)
    if fmt == "e4m3":
        byte = np.frexp(amax)[1] - 1 + 127 - 7
    else:
        mant, ex = np.frexp(amax / 6.0)
        byte = np.where(mant > 0.5, ex, ex - 1) + 127
    byte = np.clip(np.where(amax > 0, byte, 1), 1, 254)
    scaled = (w * np.exp2(127.0 - byte)[:, None, :]).reshape(k, n).astype(np.float32)
    by_word = np.ascontiguousarray(scaled.reshape(k // 512, 128, 4, n).transpose(0, 1, 3, 2))
    if fmt == "e4m3":
        words = by_word.astype(ml_dtypes.float8_e4m3fn).view(np.uint8)
    else:
        c = by_word.astype(ml_dtypes.float4_e2m1fn).view(np.uint8) & 0xF
        words = (c[..., 0::2] | (c[..., 1::2] << 4)).reshape(k // 512, 128, 2 * n)
    return np.ascontiguousarray(words), np.ascontiguousarray(byte.astype(np.uint8).reshape(k // 512, 16, n))


def unpack_weight(words, scales, fmt):
    g, _, n = scales.shape
    words = np.ascontiguousarray(words).reshape(g, 128, n, -1)
    if fmt == "e4m3":
        vals = words.view(ml_dtypes.float8_e4m3fn).astype(np.float64)
    else:
        nib = np.empty((g, 128, n, 4), np.uint8)
        nib[..., 0::2] = words & 0xF
        nib[..., 1::2] = words >> 4
        vals = E2M1[nib]
    vals = vals * np.repeat(np.exp2(scales.astype(np.float64) - 127.0), 8, axis=1)[..., None]
    return vals.transpose(0, 1, 3, 2).reshape(g * 512, n)


K, T, J, R, O, N, E = 512, 2048, 256, 512, 128, 256, 1024


def setup_inputs():
    n = np.random.standard_normal
    idx = np.random.permutation(T)[:J]
    idx2 = np.random.permutation(T)[:J]
    idx3 = np.random.permutation(T)[:J]
    idx4 = np.random.permutation(J)[:O]
    idx5 = np.random.permutation(J)[:O]
    idx6 = np.random.permutation(E)[:O]
    fk = mx_kscale(K)
    fr = mx_kscale(R)
    xtp = pack_weight(n((K, T)) / fk[:, None], "e2m1")
    wp = pack_weight(n((K, R)) * 1 / np.sqrt(K) * fk[:, None] * fr, "e4m3")
    wbp = pack_weight(n((R, N)) * 1 / np.sqrt(R) / fr[:, None], "e2m1")
    return {
        "xt_words": xtp[0],
        "xt_scales": xtp[1],
        "w_words": wp[0],
        "w_scales": wp[1],
        "wb_words": wbp[0],
        "wb_scales": wbp[1],
        "offs": striped(idx),
        "offs2": striped(idx2),
        "offs3": striped(idx3),
        "offs4": striped(idx4),
        "offs5": striped(idx5),
        "offs6": striped(idx6),
    }


def reference(xt_words, xt_scales, w_words, w_scales, wb_words, wb_scales, offs, offs2, offs3, offs4, offs5, offs6):
    idx = unstriped(offs)
    idx2 = unstriped(offs2)
    idx3 = unstriped(offs3)
    idx4 = unstriped(offs4)
    idx5 = unstriped(offs5)
    idx6 = unstriped(offs6)
    xtu = unpack_weight(xt_words, xt_scales, "e2m1")
    wu = unpack_weight(w_words, w_scales, "e4m3")
    wbu = unpack_weight(wb_words, wb_scales, "e2m1")
    xtidxg = xtu[:, idx]
    a = wu.T @ xtidxg
    xtidx2g = xtu[:, idx2]
    b = wu.T @ xtidx2g
    xtidx3g = xtu[:, idx3]
    g0 = wu.T @ xtidx3g
    c1 = np.maximum(b, g0)
    hid = np.abs(a[:, idx4] - c1[:, idx5])
    hidq = mxq(hid, 0, "e5m2")
    p = wbu.T @ hidq
    y = np.zeros((N, E))
    y[:, idx6] = p
    return y

@@ -1,0 +1,140 @@
+from contextlib import ExitStack
+
+import concourse.mybir as mybir
+
+F32 = mybir.dt.float32
+BF16 = mybir.dt.bfloat16
+I32 = mybir.dt.int32
+U32 = mybir.dt.uint32
+U16 = mybir.dt.uint16
+U8 = mybir.dt.uint8
+E4M3X4 = mybir.dt.float8_e4m3fn_x4
+E5M2X4 = mybir.dt.float8_e5m2_x4
+E2M1X4 = mybir.dt.float4_e2m1fn_x4
+ACT = mybir.ActivationFunctionType
+ALU = mybir.AluOpType
+
+P = 128
+K, T, J, R, O, N, E = 512, 2048, 256, 512, 128, 256, 1024
+PACK = 4
+FLOPS = 2 * K * R * J * 3 + 2 * R * N * O
+
+
+def load_scale_rows(queue, plane, rows):
+    for q in range(4):
+        queue.dma_start(out=plane[32 * q : 32 * q + 4, :].bitcast(I32), in_=rows[4 * q : 4 * q + 4, :].bitcast(I32))
+
+
+def tile_list_triple_looked_one_scattered_kernel(
+    tc, xt_words, xt_scales, w_words, w_scales, wb_words, wb_scales, offs, offs2, offs3, offs4, offs5, offs6, out
+):
+    nc = tc.nc
+    with ExitStack() as ctx:
+        sb = ctx.enter_context(tc.tile_pool(name="sb", bufs=1))
+        ps = ctx.enter_context(tc.psum_pool(name="ps", bufs=1))
+
+        tok_list = [sb.tile([P, J // 16], U16, name="tok_list%d" % i) for i in range(3)]
+        a_list = sb.tile([P, O // 16], U16, name="a_list")
+        c_list = sb.tile([P, O // 16], U16, name="c_list")
+        page_list = sb.tile([P, O // 16], U16, name="page_list")
+        xw = sb.tile([P, T], U16, name="xw", align_bytes=64)
+        xs = sb.tile([P, T], U8, name="xs", align_bytes=64)
+        ww = sb.tile([P, R], U32, name="ww", align_bytes=64)
+        ws = sb.tile([P, R], U8, name="ws", align_bytes=64)
+        wbw = sb.tile([P, 2 * N], U8, name="wbw", align_bytes=64)
+        wbs = sb.tile([P, N], U8, name="wbs", align_bytes=64)
+        page = [sb.tile([P, E], F32, name="page%d" % h) for h in range(2)]
+
+        nc.vector.memset(xs[:].bitcast(I32), 0)
+        nc.vector.memset(ws[:].bitcast(I32), 0)
+        nc.vector.memset(wbs[:].bitcast(I32), 0)
+        for h in range(2):
+            nc.vector.memset(page[h][:], 0.0)
+
+        nc.sync.dma_start(tok_list[0][:], offs)
+        load_scale_rows(nc.sync, xs, xt_scales[0])
+        nc.sync.dma_start(out=xw[:].bitcast(I32), in_=xt_words[0].bitcast(I32))
+        nc.sync.dma_start(tok_list[1][:], offs2)
+        nc.sync.dma_start(out=ww[:].bitcast(I32), in_=w_words[0].rearrange("p n t -> p (n t)").bitcast(I32))
+        nc.sync.dma_start(tok_list[2][:], offs3)
+        load_scale_rows(nc.sync, ws, w_scales[0])
+        nc.sync.dma_start(a_list[:], offs4)
+        nc.sync.dma_start(c_list[:], offs5)
+        nc.sync.dma_start(out=wbw[:].bitcast(I32), in_=wb_words[0].bitcast(I32))
+        load_scale_rows(nc.sync, wbs, wb_scales[0])
+        nc.sync.dma_start(page_list[:], offs6)
+
+        gw = [sb.tile([P, J], U16, name="gw%d" % i, align_bytes=64) for i in range(3)]
+        gs = [sb.tile([P, J], U8, name="gs%d" % i, align_bytes=64) for i in range(3)]
+        wwp = sb.tile([P, R], U32, name="wwp", align_bytes=64)
+        wsp = sb.tile([P, R], U8, name="wsp", align_bytes=64)
+
+        def gather_tokens(i):
+            nc.vector.tensor_copy(gs[i][:], xs[:].indirect(tok_list[i][:]))
+            nc.vector.tensor_copy(gw[i][:], xw[:].indirect(tok_list[i][:]))
+
+        def first_product(i, t, dst):
+            cols = slice(t * P, (t + 1) * P)
+            nc.tensor.matmul_mx(
+                out=dst, lhsT=wwp[:, cols].bitcast(E4M3X4), lhsT_scale=wsp[:, cols],
+                rhs=gw[i][:].bitcast(E2M1X4), rhs_scale=gs[i][:], start=True, stop=True,
+            )
+
+        gather_tokens(0)
+        nc.vector.tensor_copy(wwp[:].rearrange("p (t q) -> p q t", t=PACK), ww[:].rearrange("p (q t) -> p q t", t=PACK))
+        nc.vector.tensor_copy(wsp[:].rearrange("p (t q) -> p t q", t=PACK), ws[:].rearrange("p (q t) -> p t q", t=PACK))
+        gather_tokens(1)
+        gather_tokens(2)
+
+        a_ps = [ps.tile([P, 2 * J], F32, name="a_ps%d" % u, tag="bank%d" % u) for u in range(2)]
+        b_ps = [ps.tile([P, 2 * J], F32, name="b_ps%d" % u) for u in range(2)]
+        g_ps = [ps.tile([P, J], F32, name="g_ps%d" % t) for t in range(PACK)]
+        a_sb = [sb.tile([P, 2 * J], F32, name="a_sb%d" % u) for u in range(2)]
+        b_sb = [sb.tile([P, 2 * J], F32, name="b_sb%d" % u) for u in range(2)]
+        c_sb = [sb.tile([P, J], F32, name="c_sb%d" % t) for t in range(PACK)]
+        a_pick = sb.tile([P, PACK, O], F32, name="a_pick")
+        diff = sb.tile([P, PACK, O], F32, name="diff")
+
+        def half(t):
+            return slice((t % 2) * J, (t % 2 + 1) * J)
+
+        for u in range(2):
+            for t in (2 * u, 2 * u + 1):
+                first_product(0, t, a_ps[u][:, half(t)])
+            nc.scalar.activation(a_sb[u][:], a_ps[u][:], ACT.Copy)
+        for u in range(2):
+            for t in (2 * u, 2 * u + 1):
+                first_product(1, t, b_ps[u][:, half(t)])
+            nc.scalar.activation(b_sb[u][:], b_ps[u][:], ACT.Copy)
+        for t in range(PACK):
+            first_product(2, t, g_ps[t][:])
+        for t in range(PACK):
+            nc.scalar.activation(a_pick[:, t, :], a_sb[t // 2][:, half(t)].indirect(a_list[:]), ACT.Copy)
+        for t in range(PACK):
+            nc.vector.tensor_tensor(c_sb[t][:], g_ps[t][:], b_sb[t // 2][:, half(t)], ALU.max)
+        for t in range(PACK):
+            nc.vector.tensor_tensor(diff[:, t, :], c_sb[t][:].indirect(c_list[:]), a_pick[:, t, :], ALU.subtract)
+
+        hid = sb.tile([P, O, PACK], BF16, name="hid", align_bytes=64)
+        hq = sb.tile([P, O], U32, name="hq", align_bytes=64)
+        hs = sb.tile([P, O], U8, name="hs", align_bytes=64)
+        nc.scalar.activation(
+            hid[:].rearrange("p (c i) t -> p c t i", i=4), diff[:].rearrange("p t (c i) -> p c t i", i=4), ACT.Abs
+        )
+        nc.vector.quantize_mx(out=hq[:].bitcast(E5M2X4), scales=hs[:], in_=hid[:].rearrange("p o t -> p (o t)"))
+
+        p_sb = [sb.tile([P, O], F32, name="p_sb%d" % h) for h in range(2)]
+        for h in range(2):
+            p_ps = ps.tile([P, 2 * J], F32, name="p_ps%d" % h, tag="bank%d" % h)
+            nc.tensor.matmul_mx(
+                out=p_ps[:, 0:O], lhsT=wbw[:, 2 * P * h : 2 * P * (h + 1)].bitcast(E2M1X4), lhsT_scale=wbs[:, P * h : P * (h + 1)],
+                rhs=hq[:].bitcast(E5M2X4), rhs_scale=hs[:], start=True, stop=True,
+            )
+            if h == 0:
+                nc.vector.tensor_copy(p_sb[h][:], p_ps[:, 0:O])
+                nc.vector.tensor_copy(page[h][:].indirect(page_list[:]), p_sb[h][:])
+                nc.sync.dma_start(out=out[P * h : P * (h + 1), :], in_=page[h][:])
+            else:
+                nc.scalar.activation(p_sb[h][:], p_ps[:, 0:O], ACT.Copy)
+                nc.scalar.activation(page[h][:].indirect(page_list[:]), p_sb[h][:], ACT.Copy)
+                nc.scalar.dma_start(out=out[P * h : P * (h + 1), :], in_=page[h][:])

@@ -20,8 +20,8 @@ PACK = 4
 FLOPS = 2 * K * R * J * 3 + 2 * R * N * O
 
 
-def load_scale_rows(queue, plane, rows):
-    for q in range(4):
+def load_scale_rows(queue, plane, rows, quadrants=range(4)):
+    for q in quadrants:
         queue.dma_start(out=plane[32 * q : 32 * q + 4, :].bitcast(I32), in_=rows[4 * q : 4 * q + 4, :].bitcast(I32))
 
 
@@ -31,101 +31,115 @@ def tile_list_triple_looked_one_scattered_kernel(
     nc = tc.nc
     with ExitStack() as ctx:
         sb = ctx.enter_context(tc.tile_pool(name="sb", bufs=1))
+        lap = ctx.enter_context(tc.tile_pool(name="lap", bufs=1))
         ps = ctx.enter_context(tc.psum_pool(name="ps", bufs=1))
 
         tok_list = [sb.tile([P, J // 16], U16, name="tok_list%d" % i) for i in range(3)]
         a_list = sb.tile([P, O // 16], U16, name="a_list")
         c_list = sb.tile([P, O // 16], U16, name="c_list")
         page_list = sb.tile([P, O // 16], U16, name="page_list")
-        xw = sb.tile([P, T], U16, name="xw", align_bytes=64)
-        xs = sb.tile([P, T], U8, name="xs", align_bytes=64)
-        ww = sb.tile([P, R], U32, name="ww", align_bytes=64)
-        ws = sb.tile([P, R], U8, name="ws", align_bytes=64)
+        xw = sb.tile([P, T], U16, name="xw", tag="xw", align_bytes=64)
+        xs = sb.tile([P, T], U8, name="xs", tag="xs", align_bytes=64)
+        ww = sb.tile([P, R], U32, name="ww", tag="ww", align_bytes=64)
+        ws = lap.tile([P, R], U8, name="ws", align_bytes=64, offset=768)
         wbw = sb.tile([P, 2 * N], U8, name="wbw", align_bytes=64)
         wbs = sb.tile([P, N], U8, name="wbs", align_bytes=64)
-        page = [sb.tile([P, E], F32, name="page%d" % h) for h in range(2)]
 
         nc.vector.memset(xs[:].bitcast(I32), 0)
         nc.vector.memset(ws[:].bitcast(I32), 0)
         nc.vector.memset(wbs[:].bitcast(I32), 0)
-        for h in range(2):
-            nc.vector.memset(page[h][:], 0.0)
 
         nc.sync.dma_start(tok_list[0][:], offs)
-        load_scale_rows(nc.sync, xs, xt_scales[0])
-        nc.sync.dma_start(out=xw[:].bitcast(I32), in_=xt_words[0].bitcast(I32))
         nc.sync.dma_start(tok_list[1][:], offs2)
+        load_scale_rows(nc.sync, xs, xt_scales[0], (0, 1))
+        load_scale_rows(nc.scalar, xs, xt_scales[0], (2, 3))
+        nc.sync.dma_start(out=xw[:].bitcast(I32), in_=xt_words[0].bitcast(I32))
         nc.sync.dma_start(out=ww[:].bitcast(I32), in_=w_words[0].rearrange("p n t -> p (n t)").bitcast(I32))
-        nc.sync.dma_start(tok_list[2][:], offs3)
         load_scale_rows(nc.sync, ws, w_scales[0])
+        nc.sync.dma_start(tok_list[2][:], offs3)
         nc.sync.dma_start(a_list[:], offs4)
         nc.sync.dma_start(c_list[:], offs5)
         nc.sync.dma_start(out=wbw[:].bitcast(I32), in_=wb_words[0].bitcast(I32))
         load_scale_rows(nc.sync, wbs, wb_scales[0])
         nc.sync.dma_start(page_list[:], offs6)
 
-        gw = [sb.tile([P, J], U16, name="gw%d" % i, align_bytes=64) for i in range(3)]
-        gs = [sb.tile([P, J], U8, name="gs%d" % i, align_bytes=64) for i in range(3)]
+        gw0 = sb.tile([P, J], U16, name="gw0", align_bytes=64)
+        gs0 = sb.tile([P, J], U8, name="gs0", align_bytes=64)
+        gw12 = lap.tile([P, 2 * J], U16, name="gw12", align_bytes=64, offset=0)
+        gs1 = sb.tile([P, J], U8, name="gs1", align_bytes=64)
+        gs2 = lap.tile([P, J], U8, name="gs2", align_bytes=64, offset=1024)
+        gw = [gw0[:], gw12[:, 0:J], gw12[:, J : 2 * J]]
+        gs = [gs0[:], gs1[:], gs2[:]]
         wwp = sb.tile([P, R], U32, name="wwp", align_bytes=64)
         wsp = sb.tile([P, R], U8, name="wsp", align_bytes=64)
 
         def gather_tokens(i):
-            nc.vector.tensor_copy(gs[i][:], xs[:].indirect(tok_list[i][:]))
-            nc.vector.tensor_copy(gw[i][:], xw[:].indirect(tok_list[i][:]))
+            nc.vector.tensor_copy(gs[i], xs[:].indirect(tok_list[i][:]))
+            nc.vector.tensor_copy(gw[i], xw[:].indirect(tok_list[i][:]))
 
         def first_product(i, t, dst):
             cols = slice(t * P, (t + 1) * P)
             nc.tensor.matmul_mx(
                 out=dst, lhsT=wwp[:, cols].bitcast(E4M3X4), lhsT_scale=wsp[:, cols],
-                rhs=gw[i][:].bitcast(E2M1X4), rhs_scale=gs[i][:], start=True, stop=True,
+                rhs=gw[i].bitcast(E2M1X4), rhs_scale=gs[i], start=True, stop=True,
             )
 
         gather_tokens(0)
-        nc.vector.tensor_copy(wwp[:].rearrange("p (t q) -> p q t", t=PACK), ww[:].rearrange("p (q t) -> p q t", t=PACK))
+        nc.scalar.copy(wwp[:].rearrange("p (t q) -> p q t", t=PACK), ww[:].rearrange("p (q t) -> p q t", t=PACK))
         nc.vector.tensor_copy(wsp[:].rearrange("p (t q) -> p t q", t=PACK), ws[:].rearrange("p (q t) -> p t q", t=PACK))
         gather_tokens(1)
         gather_tokens(2)
+        page = [sb.tile([P, E], F32, name="page%d" % h, tag=("xs", "ww")[h], align_bytes=64) for h in range(2)]
+        for h in (1, 0):
+            nc.gpsimd.memset(page[h][:], 0.0)
 
-        a_ps = [ps.tile([P, 2 * J], F32, name="a_ps%d" % u, tag="bank%d" % u) for u in range(2)]
+        a_ps = [ps.tile([P, 2 * J], F32, name="a_ps%d" % u, tag="bank%d" % u) for u in range(3)]
         b_ps = [ps.tile([P, 2 * J], F32, name="b_ps%d" % u) for u in range(2)]
-        g_ps = [ps.tile([P, J], F32, name="g_ps%d" % t) for t in range(PACK)]
         a_sb = [sb.tile([P, 2 * J], F32, name="a_sb%d" % u) for u in range(2)]
         b_sb = [sb.tile([P, 2 * J], F32, name="b_sb%d" % u) for u in range(2)]
         c_sb = [sb.tile([P, J], F32, name="c_sb%d" % t) for t in range(PACK)]
-        a_pick = sb.tile([P, PACK, O], F32, name="a_pick")
+        a_pick = sb.tile([P, PACK, O], F32, name="a_pick", tag="xw", align_bytes=64)
+        c_pick = sb.tile([P, PACK - 1, O], F32, name="c_pick")
         diff = sb.tile([P, PACK, O], F32, name="diff")
 
         def half(t):
             return slice((t % 2) * J, (t % 2 + 1) * J)
 
-        for u in range(2):
-            for t in (2 * u, 2 * u + 1):
-                first_product(0, t, a_ps[u][:, half(t)])
-            nc.scalar.activation(a_sb[u][:], a_ps[u][:], ACT.Copy)
+        for t in (0, 1):
+            first_product(0, t, a_ps[t][:, 0:J])
+            nc.scalar.activation(a_sb[0][:, half(t)], a_ps[t][:, 0:J], ACT.Copy)
+        for t in (2, 3):
+            first_product(0, t, a_ps[2][:, half(t)])
+        nc.scalar.activation(a_sb[1][:], a_ps[2][:], ACT.Copy)
         for u in range(2):
             for t in (2 * u, 2 * u + 1):
                 first_product(1, t, b_ps[u][:, half(t)])
             nc.scalar.activation(b_sb[u][:], b_ps[u][:], ACT.Copy)
+        g_ps = [ps.tile([P, J], F32, name="g_ps%d" % t, tag=("g0", "g1", "g2", "bank0")[t]) for t in range(PACK)]
         for t in range(PACK):
             first_product(2, t, g_ps[t][:])
-        for t in range(PACK):
-            nc.scalar.activation(a_pick[:, t, :], a_sb[t // 2][:, half(t)].indirect(a_list[:]), ACT.Copy)
+        for t in (0, 1):
+            nc.vector.tensor_copy(a_pick[:, t, :], a_sb[0][:, half(t)].indirect(a_list[:]))
+        for t in (2, 3):
+            nc.scalar.activation(a_pick[:, t, :], a_sb[1][:, half(t)].indirect(a_list[:]), ACT.Copy)
         for t in range(PACK):
             nc.vector.tensor_tensor(c_sb[t][:], g_ps[t][:], b_sb[t // 2][:, half(t)], ALU.max)
-        for t in range(PACK):
-            nc.vector.tensor_tensor(diff[:, t, :], c_sb[t][:].indirect(c_list[:]), a_pick[:, t, :], ALU.subtract)
+        for t in range(PACK - 1):
+            nc.scalar.activation(c_pick[:, t, :], c_sb[t][:].indirect(c_list[:]), ACT.Copy)
+        nc.vector.tensor_tensor(diff[:, 3, :], c_sb[3][:].indirect(c_list[:]), a_pick[:, 3, :], ALU.subtract)
+        nc.vector.tensor_tensor(diff[:, 0:2, :], c_pick[:, 0:2, :], a_pick[:, 0:2, :], ALU.subtract)
+        nc.vector.tensor_tensor(diff[:, 2, :], c_pick[:, 2, :], a_pick[:, 2, :], ALU.subtract)
 
         hid = sb.tile([P, O, PACK], BF16, name="hid", align_bytes=64)
         hq = sb.tile([P, O], U32, name="hq", align_bytes=64)
         hs = sb.tile([P, O], U8, name="hs", align_bytes=64)
-        nc.scalar.activation(
-            hid[:].rearrange("p (c i) t -> p c t i", i=4), diff[:].rearrange("p t (c i) -> p c t i", i=4), ACT.Abs
-        )
+        for pair in (slice(0, 2), slice(2, 4)):
+            nc.scalar.activation(hid[:, :, pair], diff[:, pair, :].rearrange("p t o -> p o t"), ACT.Abs)
         nc.vector.quantize_mx(out=hq[:].bitcast(E5M2X4), scales=hs[:], in_=hid[:].rearrange("p o t -> p (o t)"))
 
         p_sb = [sb.tile([P, O], F32, name="p_sb%d" % h) for h in range(2)]
         for h in range(2):
-            p_ps = ps.tile([P, 2 * J], F32, name="p_ps%d" % h, tag="bank%d" % h)
+            p_ps = ps.tile([P, 2 * J], F32, name="p_ps%d" % h, tag="bank%d" % (h + 1))
             nc.tensor.matmul_mx(
                 out=p_ps[:, 0:O], lhsT=wbw[:, 2 * P * h : 2 * P * (h + 1)].bitcast(E2M1X4), lhsT_scale=wbs[:, P * h : P * (h + 1)],
                 rhs=hq[:].bitcast(E5M2X4), rhs_scale=hs[:], start=True, stop=True,

@@ -39,8 +39,8 @@ def tile_list_triple_looked_one_scattered_kernel(
         c_list = sb.tile([P, O // 16], U16, name="c_list")
         page_list = sb.tile([P, O // 16], U16, name="page_list")
         xw = sb.tile([P, T], U16, name="xw", tag="xw", align_bytes=64)
-        xs = sb.tile([P, T], U8, name="xs", tag="xs", align_bytes=64)
-        ww = sb.tile([P, R], U32, name="ww", tag="ww", align_bytes=64)
+        xs = sb.tile([P, T], U8, name="xs", align_bytes=64)
+        ww = sb.tile([P, R], U32, name="ww", align_bytes=64)
         ws = lap.tile([P, R], U8, name="ws", align_bytes=64, offset=768)
         wbw = sb.tile([P, 2 * N], U8, name="wbw", align_bytes=64)
         wbs = sb.tile([P, N], U8, name="wbs", align_bytes=64)
@@ -48,6 +48,9 @@ def tile_list_triple_looked_one_scattered_kernel(
         nc.vector.memset(xs[:].bitcast(I32), 0)
         nc.vector.memset(ws[:].bitcast(I32), 0)
         nc.vector.memset(wbs[:].bitcast(I32), 0)
+        page = [sb.tile([P, E], F32, name="page%d" % h) for h in range(2)]
+        for h in range(2):
+            nc.vector.memset(page[h][:], 0.0)
 
         nc.sync.dma_start(tok_list[0][:], offs)
         nc.sync.dma_start(tok_list[1][:], offs2)
@@ -89,9 +92,6 @@ def tile_list_triple_looked_one_scattered_kernel(
         nc.vector.tensor_copy(wsp[:].rearrange("p (t q) -> p t q", t=PACK), ws[:].rearrange("p (q t) -> p t q", t=PACK))
         gather_tokens(1)
         gather_tokens(2)
-        page = [sb.tile([P, E], F32, name="page%d" % h, tag=("xs", "ww")[h], align_bytes=64) for h in range(2)]
-        for h in (1, 0):
-            nc.gpsimd.memset(page[h][:], 0.0)
 
         a_ps = [ps.tile([P, 2 * J], F32, name="a_ps%d" % u, tag="bank%d" % u) for u in range(3)]
         b_ps = [ps.tile([P, 2 * J], F32, name="b_ps%d" % u) for u in range(2)]
@@ -99,7 +99,7 @@ def tile_list_triple_looked_one_scattered_kernel(
         b_sb = [sb.tile([P, 2 * J], F32, name="b_sb%d" % u) for u in range(2)]
         c_sb = [sb.tile([P, J], F32, name="c_sb%d" % t) for t in range(PACK)]
         a_pick = sb.tile([P, PACK, O], F32, name="a_pick", tag="xw", align_bytes=64)
-        c_pick = sb.tile([P, PACK - 1, O], F32, name="c_pick")
+        c_pick = sb.tile([P, 2, O], F32, name="c_pick")
         diff = sb.tile([P, PACK, O], F32, name="diff")
 
         def half(t):
@@ -124,16 +124,16 @@ def tile_list_triple_looked_one_scattered_kernel(
             nc.scalar.activation(a_pick[:, t, :], a_sb[1][:, half(t)].indirect(a_list[:]), ACT.Copy)
         for t in range(PACK):
             nc.vector.tensor_tensor(c_sb[t][:], g_ps[t][:], b_sb[t // 2][:, half(t)], ALU.max)
-        for t in range(PACK - 1):
+        for t in (0, 1):
             nc.scalar.activation(c_pick[:, t, :], c_sb[t][:].indirect(c_list[:]), ACT.Copy)
-        nc.vector.tensor_tensor(diff[:, 3, :], c_sb[3][:].indirect(c_list[:]), a_pick[:, 3, :], ALU.subtract)
-        nc.vector.tensor_tensor(diff[:, 0:2, :], c_pick[:, 0:2, :], a_pick[:, 0:2, :], ALU.subtract)
-        nc.vector.tensor_tensor(diff[:, 2, :], c_pick[:, 2, :], a_pick[:, 2, :], ALU.subtract)
+        for t in (2, 3):
+            nc.vector.tensor_tensor(diff[:, t, :], c_sb[t][:].indirect(c_list[:]), a_pick[:, t, :], ALU.subtract)
+        nc.vector.tensor_tensor(diff[:, 0:2, :], c_pick[:], a_pick[:, 0:2, :], ALU.subtract)
 
         hid = sb.tile([P, O, PACK], BF16, name="hid", align_bytes=64)
         hq = sb.tile([P, O], U32, name="hq", align_bytes=64)
         hs = sb.tile([P, O], U8, name="hs", align_bytes=64)
-        for pair in (slice(0, 2), slice(2, 4)):
+        for pair in (slice(2, 4), slice(0, 2)):
             nc.scalar.activation(hid[:, :, pair], diff[:, pair, :].rearrange("p t o -> p o t"), ACT.Abs)
         nc.vector.quantize_mx(out=hq[:].bitcast(E5M2X4), scales=hs[:], in_=hid[:].rearrange("p o t -> p (o t)"))
 

@@ -97,7 +97,7 @@ def tile_list_triple_looked_one_scattered_kernel(
         b_ps = [ps.tile([P, 2 * J], F32, name="b_ps%d" % u) for u in range(2)]
         a_sb = [sb.tile([P, 2 * J], F32, name="a_sb%d" % u) for u in range(2)]
         b_sb = [sb.tile([P, 2 * J], F32, name="b_sb%d" % u) for u in range(2)]
-        c_sb = [sb.tile([P, J], F32, name="c_sb%d" % t) for t in range(PACK)]
+        c_sb = [sb.tile([P, 2 * J], F32, name="c_sb%d" % u) for u in range(2)]
         a_pick = sb.tile([P, PACK, O], F32, name="a_pick", tag="xw", align_bytes=64)
         c_pick = sb.tile([P, 2, O], F32, name="c_pick")
         diff = sb.tile([P, PACK, O], F32, name="diff")
@@ -112,29 +112,33 @@ def tile_list_triple_looked_one_scattered_kernel(
             first_product(0, t, a_ps[2][:, half(t)])
         nc.scalar.activation(a_sb[1][:], a_ps[2][:], ACT.Copy)
         for u in range(2):
-            for t in (2 * u, 2 * u + 1):
-                first_product(1, t, b_ps[u][:, half(t)])
+            first_product(1, u + 2, b_ps[u][:, 0:J])
+            first_product(1, u, b_ps[u][:, J : 2 * J])
             nc.scalar.activation(b_sb[u][:], b_ps[u][:], ACT.Copy)
-        g_ps = [ps.tile([P, J], F32, name="g_ps%d" % t, tag=("g0", "g1", "g2", "bank0")[t]) for t in range(PACK)]
-        for t in range(PACK):
-            first_product(2, t, g_ps[t][:])
+        g_ps = [ps.tile([P, 2 * J], F32, name="g_ps%d" % u) for u in range(2)]
+        for u in range(2):
+            first_product(2, u + 2, g_ps[u][:, 0:J])
+            first_product(2, u, g_ps[u][:, J : 2 * J])
         for t in (0, 1):
             nc.vector.tensor_copy(a_pick[:, t, :], a_sb[0][:, half(t)].indirect(a_list[:]))
         for t in (2, 3):
             nc.scalar.activation(a_pick[:, t, :], a_sb[1][:, half(t)].indirect(a_list[:]), ACT.Copy)
-        for t in range(PACK):
-            nc.vector.tensor_tensor(c_sb[t][:], g_ps[t][:], b_sb[t // 2][:, half(t)], ALU.max)
+        for u in range(2):
+            nc.vector.tensor_tensor(c_sb[u][:], g_ps[u][:], b_sb[u][:], ALU.max)
         for t in (0, 1):
-            nc.scalar.activation(c_pick[:, t, :], c_sb[t][:].indirect(c_list[:]), ACT.Copy)
+            nc.scalar.activation(c_pick[:, t, :], c_sb[t][:, J : 2 * J].indirect(c_list[:]), ACT.Copy)
         for t in (2, 3):
-            nc.vector.tensor_tensor(diff[:, t, :], c_sb[t][:].indirect(c_list[:]), a_pick[:, t, :], ALU.subtract)
-        nc.vector.tensor_tensor(diff[:, 0:2, :], c_pick[:], a_pick[:, 0:2, :], ALU.subtract)
+            nc.vector.tensor_tensor(diff[:, t, :], c_sb[t - 2][:].indirect(c_list[:]), a_pick[:, t, :], ALU.subtract)
+        for places in (slice(64, O), slice(0, 64)):
+            nc.vector.tensor_tensor(diff[:, 0:2, places], c_pick[:, :, places], a_pick[:, 0:2, places], ALU.subtract)
 
         hid = sb.tile([P, O, PACK], BF16, name="hid", align_bytes=64)
         hq = sb.tile([P, O], U32, name="hq", align_bytes=64)
         hs = sb.tile([P, O], U8, name="hs", align_bytes=64)
-        for pair in (slice(2, 4), slice(0, 2)):
-            nc.scalar.activation(hid[:, :, pair], diff[:, pair, :].rearrange("p t o -> p o t"), ACT.Abs)
+        nc.scalar.activation(hid[:, :, 2:4], diff[:, 2:4, :].rearrange("p t o -> p o t"), ACT.Abs)
+        nc.scalar.activation(hid[:, 0:64, 0:2], diff[:, 0:2, 0:64].rearrange("p t o -> p o t"), ACT.Abs)
+        upper = diff[:, 0:2, 64:O].rearrange("p t o -> p o t")
+        nc.vector.scalar_tensor_tensor(hid[:, 64:O, 0:2], upper, -1.0, upper, ALU.mult, ALU.max)
         nc.vector.quantize_mx(out=hq[:].bitcast(E5M2X4), scales=hs[:], in_=hid[:].rearrange("p o t -> p (o t)"))
 
         p_sb = [sb.tile([P, O], F32, name="p_sb%d" % h) for h in range(2)]

from contextlib import ExitStack

import concourse.mybir as mybir

F32 = mybir.dt.float32
BF16 = mybir.dt.bfloat16
I32 = mybir.dt.int32
U32 = mybir.dt.uint32
U16 = mybir.dt.uint16
U8 = mybir.dt.uint8
E4M3X4 = mybir.dt.float8_e4m3fn_x4
E5M2X4 = mybir.dt.float8_e5m2_x4
E2M1X4 = mybir.dt.float4_e2m1fn_x4
ACT = mybir.ActivationFunctionType
ALU = mybir.AluOpType

P = 128
K, T, J, R, O, N, E = 512, 2048, 256, 512, 128, 256, 1024
PACK = 4
FLOPS = 2 * K * R * J * 3 + 2 * R * N * O


def load_scale_rows(queue, plane, rows, quadrants=range(4)):
    for q in quadrants:
        queue.dma_start(out=plane[32 * q : 32 * q + 4, :].bitcast(I32), in_=rows[4 * q : 4 * q + 4, :].bitcast(I32))


def tile_list_triple_looked_one_scattered_kernel(
    tc, xt_words, xt_scales, w_words, w_scales, wb_words, wb_scales, offs, offs2, offs3, offs4, offs5, offs6, out
):
    nc = tc.nc
    with ExitStack() as ctx:
        sb = ctx.enter_context(tc.tile_pool(name="sb", bufs=1))
        lap = ctx.enter_context(tc.tile_pool(name="lap", bufs=1))
        ps = ctx.enter_context(tc.psum_pool(name="ps", bufs=1))

        tok_list = [sb.tile([P, J // 16], U16, name="tok_list%d" % i) for i in range(3)]
        a_list = sb.tile([P, O // 16], U16, name="a_list")
        c_list = sb.tile([P, O // 16], U16, name="c_list")
        page_list = sb.tile([P, O // 16], U16, name="page_list")
        xw = sb.tile([P, T], U16, name="xw", tag="xw", align_bytes=64)
        xs = sb.tile([P, T], U8, name="xs", align_bytes=64)
        ww = sb.tile([P, R], U32, name="ww", align_bytes=64)
        ws = lap.tile([P, R], U8, name="ws", align_bytes=64, offset=768)
        wbw = sb.tile([P, 2 * N], U8, name="wbw", align_bytes=64)
        wbs = sb.tile([P, N], U8, name="wbs", align_bytes=64)

        nc.vector.memset(xs[:].bitcast(I32), 0)
        nc.vector.memset(ws[:].bitcast(I32), 0)
        nc.vector.memset(wbs[:].bitcast(I32), 0)
        page = [sb.tile([P, E], F32, name="page%d" % h) for h in range(2)]
        for h in range(2):
            nc.vector.memset(page[h][:], 0.0)

        nc.sync.dma_start(tok_list[0][:], offs)
        nc.sync.dma_start(tok_list[1][:], offs2)
        load_scale_rows(nc.sync, xs, xt_scales[0], (0, 1))
        load_scale_rows(nc.scalar, xs, xt_scales[0], (2, 3))
        nc.sync.dma_start(out=xw[:].bitcast(I32), in_=xt_words[0].bitcast(I32))
        nc.sync.dma_start(out=ww[:].bitcast(I32), in_=w_words[0].rearrange("p n t -> p (n t)").bitcast(I32))
        load_scale_rows(nc.sync, ws, w_scales[0])
        nc.sync.dma_start(tok_list[2][:], offs3)
        nc.sync.dma_start(a_list[:], offs4)
        nc.sync.dma_start(c_list[:], offs5)
        nc.sync.dma_start(out=wbw[:].bitcast(I32), in_=wb_words[0].bitcast(I32))
        load_scale_rows(nc.sync, wbs, wb_scales[0])
        nc.sync.dma_start(page_list[:], offs6)

        gw0 = sb.tile([P, J], U16, name="gw0", align_bytes=64)
        gs0 = sb.tile([P, J], U8, name="gs0", align_bytes=64)
        gw12 = lap.tile([P, 2 * J], U16, name="gw12", align_bytes=64, offset=0)
        gs1 = sb.tile([P, J], U8, name="gs1", align_bytes=64)
        gs2 = lap.tile([P, J], U8, name="gs2", align_bytes=64, offset=1024)
        gw = [gw0[:], gw12[:, 0:J], gw12[:, J : 2 * J]]
        gs = [gs0[:], gs1[:], gs2[:]]
        wwp = sb.tile([P, R], U32, name="wwp", align_bytes=64)
        wsp = sb.tile([P, R], U8, name="wsp", align_bytes=64)

        def gather_tokens(i):
            nc.vector.tensor_copy(gs[i], xs[:].indirect(tok_list[i][:]))
            nc.vector.tensor_copy(gw[i], xw[:].indirect(tok_list[i][:]))

        def first_product(i, t, dst):
            cols = slice(t * P, (t + 1) * P)
            nc.tensor.matmul_mx(
                out=dst, lhsT=wwp[:, cols].bitcast(E4M3X4), lhsT_scale=wsp[:, cols],
                rhs=gw[i].bitcast(E2M1X4), rhs_scale=gs[i], start=True, stop=True,
            )

        gather_tokens(0)
        nc.scalar.copy(wwp[:].rearrange("p (t q) -> p q t", t=PACK), ww[:].rearrange("p (q t) -> p q t", t=PACK))
        nc.vector.tensor_copy(wsp[:].rearrange("p (t q) -> p t q", t=PACK), ws[:].rearrange("p (q t) -> p t q", t=PACK))
        gather_tokens(1)
        gather_tokens(2)

        a_ps = [ps.tile([P, 2 * J], F32, name="a_ps%d" % u, tag="bank%d" % u) for u in range(3)]
        b_ps = [ps.tile([P, 2 * J], F32, name="b_ps%d" % u) for u in range(2)]
        a_sb = [sb.tile([P, 2 * J], F32, name="a_sb%d" % u) for u in range(2)]
        b_sb = [sb.tile([P, 2 * J], F32, name="b_sb%d" % u) for u in range(2)]
        c_sb = [sb.tile([P, 2 * J], F32, name="c_sb%d" % u) for u in range(2)]
        a_pick = sb.tile([P, PACK, O], F32, name="a_pick", tag="xw", align_bytes=64)
        c_pick = sb.tile([P, 2, O], F32, name="c_pick")
        diff = sb.tile([P, PACK, O], F32, name="diff")

        def half(t):
            return slice((t % 2) * J, (t % 2 + 1) * J)

        for t in (0, 1):
            first_product(0, t, a_ps[t][:, 0:J])
            nc.scalar.activation(a_sb[0][:, half(t)], a_ps[t][:, 0:J], ACT.Copy)
        for t in (2, 3):
            first_product(0, t, a_ps[2][:, half(t)])
        nc.scalar.activation(a_sb[1][:], a_ps[2][:], ACT.Copy)
        for u in range(2):
            first_product(1, u + 2, b_ps[u][:, 0:J])
            first_product(1, u, b_ps[u][:, J : 2 * J])
            nc.scalar.activation(b_sb[u][:], b_ps[u][:], ACT.Copy)
        g_ps = [ps.tile([P, 2 * J], F32, name="g_ps%d" % u) for u in range(2)]
        for u in range(2):
            first_product(2, u + 2, g_ps[u][:, 0:J])
            first_product(2, u, g_ps[u][:, J : 2 * J])
        for t in (0, 1):
            nc.vector.tensor_copy(a_pick[:, t, :], a_sb[0][:, half(t)].indirect(a_list[:]))
        for t in (2, 3):
            nc.scalar.activation(a_pick[:, t, :], a_sb[1][:, half(t)].indirect(a_list[:]), ACT.Copy)
        for u in range(2):
            nc.vector.tensor_tensor(c_sb[u][:], g_ps[u][:], b_sb[u][:], ALU.max)
        for t in (0, 1):
            nc.scalar.activation(c_pick[:, t, :], c_sb[t][:, J : 2 * J].indirect(c_list[:]), ACT.Copy)
        for t in (2, 3):
            nc.vector.tensor_tensor(diff[:, t, :], c_sb[t - 2][:].indirect(c_list[:]), a_pick[:, t, :], ALU.subtract)
        for places in (slice(64, O), slice(0, 64)):
            nc.vector.tensor_tensor(diff[:, 0:2, places], c_pick[:, :, places], a_pick[:, 0:2, places], ALU.subtract)

        hid = sb.tile([P, O, PACK], BF16, name="hid", align_bytes=64)
        hq = sb.tile([P, O], U32, name="hq", align_bytes=64)
        hs = sb.tile([P, O], U8, name="hs", align_bytes=64)
        nc.scalar.activation(hid[:, :, 2:4], diff[:, 2:4, :].rearrange("p t o -> p o t"), ACT.Abs)
        nc.scalar.activation(hid[:, 0:64, 0:2], diff[:, 0:2, 0:64].rearrange("p t o -> p o t"), ACT.Abs)
        upper = diff[:, 0:2, 64:O].rearrange("p t o -> p o t")
        nc.vector.scalar_tensor_tensor(hid[:, 64:O, 0:2], upper, -1.0, upper, ALU.mult, ALU.max)
        nc.vector.quantize_mx(out=hq[:].bitcast(E5M2X4), scales=hs[:], in_=hid[:].rearrange("p o t -> p (o t)"))

        p_sb = [sb.tile([P, O], F32, name="p_sb%d" % h) for h in range(2)]
        for h in range(2):
            p_ps = ps.tile([P, 2 * J], F32, name="p_ps%d" % h, tag="bank%d" % (h + 1))
            nc.tensor.matmul_mx(
                out=p_ps[:, 0:O], lhsT=wbw[:, 2 * P * h : 2 * P * (h + 1)].bitcast(E2M1X4), lhsT_scale=wbs[:, P * h : P * (h + 1)],
                rhs=hq[:].bitcast(E5M2X4), rhs_scale=hs[:], start=True, stop=True,
            )
            if h == 0:
                nc.vector.tensor_copy(p_sb[h][:], p_ps[:, 0:O])
                nc.vector.tensor_copy(page[h][:].indirect(page_list[:]), p_sb[h][:])
                nc.sync.dma_start(out=out[P * h : P * (h + 1), :], in_=page[h][:])
            else:
                nc.scalar.activation(p_sb[h][:], p_ps[:, 0:O], ACT.Copy)
                nc.scalar.activation(page[h][:].indirect(page_list[:]), p_sb[h][:], ACT.Copy)
                nc.scalar.dma_start(out=out[P * h : P * (h + 1), :], in_=page[h][:])
